import numpy as np
import ml_dtypes


def mxq(x, axis, fmt="e4m3"):
    dtype, down = {"e4m3": (ml_dtypes.float8_e4m3fn, 7), "e5m2": (ml_dtypes.float8_e5m2, 14)}[fmt]
    v = np.moveaxis(np.asarray(x, np.float32).astype(ml_dtypes.bfloat16).astype(np.float64), axis, -1)
    blocks = v.reshape(v.shape[:-1] + (-1, 32))
    amax = np.abs(blocks).max(-1, keepdims=True)
    byte = np.maximum(np.where(amax > 0, np.frexp(amax)[1] - 1 + 127, 0) - down, 1)
    scale = np.exp2(byte - 127.0)
    codes = (blocks / scale).astype(np.float32).astype(dtype).astype(np.float64)
    return np.moveaxis((codes * scale).reshape(v.shape), -1, axis)


WIDE = False


def mx_kscale(k):
    if not WIDE:
        return np.ones(k)
    levels = np.array([10, -10, 5, -5, 0])
    if k % 512:
        return np.exp2(np.random.permutation(np.resize(levels, k // 32))).repeat(32)
    a = np.empty((k // 512, 16))
    for p in range(k // 512):
        a[p, :8] = np.random.permutation(np.resize(levels, 8))
        for g in range(8):
            far = levels[np.abs(levels - a[p, g]) >= 10]
            a[p, g + 8] = far[np.random.randint(len(far))]
    return np.exp2(a.ravel()).repeat(32)


BF16 = ml_dtypes.bfloat16


def bf(x):
    return np.asarray(x, np.float32).astype(BF16)


def f64(x):
    return np.asarray(x).astype(np.float64)


E2M1 = np.array([0.0, 0.5, 1.0, 1.5, 2.0, 3.0, 4.0, 6.0, -0.0, -0.5, -1.0, -1.5, -2.0, -3.0, -4.0, -6.0])


def pack_weight(w, fmt):
    k, n = w.shape
    w = f64(bf(w)).reshape(k // 32, 32, n)
    amax = np.abs(w).max(1)
    if fmt == "e4m3":
        byte = np.frexp(amax)[1] - 1 + 127 - 7
    else:
        mant, ex = np.frexp(amax / 6.0)
        byte = np.where(mant > 0.5, ex, ex - 1) + 127
    byte = np.clip(np.where(amax > 0, byte, 1), 1, 254)
    scaled = (w * np.exp2(127.0 - byte)[:, None, :]).reshape(k, n).astype(np.float32)
    by_word = np.ascontiguousarray(scaled.reshape(k // 512, 128, 4, n).transpose(0, 1, 3, 2))
    if fmt == "e4m3":
        words = by_word.astype(ml_dtypes.float8_e4m3fn).view(np.uint8)
    else:
        c = by_word.astype(ml_dtypes.float4_e2m1fn).view(np.uint8) & 0xF
        words = c[..., 0::2] | (c[..., 1::2] << 4)
    return np.ascontiguousarray(words), np.ascontiguousarray(byte.astype(np.uint8).reshape(k // 512, 16, n))


def unpack_weight(words, scales, fmt):
    g, p, n, _ = words.shape
    if fmt == "e4m3":
        vals = np.ascontiguousarray(words).view(ml_dtypes.float8_e4m3fn).astype(np.float64)
    else:
        nib = np.empty((g, p, n, 4), np.uint8)
        nib[..., 0::2] = words & 0xF
        nib[..., 1::2] = words >> 4
        vals = E2M1[nib]
    vals = vals * np.repeat(np.exp2(scales.astype(np.float64) - 127.0), 8, axis=1)[..., None]
    return vals.transpose(0, 1, 3, 2).reshape(g * 512, n)
def pack4(w):
    words, scales = pack_weight(w, "e2m1")
    return words.reshape(words.shape[0], 128, -1), scales


def unpack4(words, scales):
    return unpack_weight(words.reshape(words.shape[0], 128, -1, 2), scales, "e2m1")


M, H, L, D = 1024, 1024, 2048, 1024


def setup_inputs():
    a, b = mx_kscale(H), mx_kscale(L)
    ab = np.concatenate([a, b])
    plan = np.maximum(np.random.standard_normal((M, H + L)), 0.0)
    f_rest_words, f_rest_scales = pack4(np.random.standard_normal((L, D)) / np.sqrt(L) / b[:, None])
    return {"plan": bf(plan * ab),
            "cost": bf(np.abs(np.random.standard_normal((M, H + L)))),
            "u": bf(0.5 + 0.5 * np.random.standard_normal(M)),
            "v": bf(0.5 + 0.5 * np.random.standard_normal(H + L)),
            "step": bf((0.75 + 0.5 * np.random.random(H + L)) * ab),
            "f_hub": bf(np.random.standard_normal((H, D)) / np.sqrt(H) / a[:, None]),
            "f_rest_words": f_rest_words,
            "f_rest_scales": f_rest_scales}


def reference(plan, cost, u, v, step, f_hub, f_rest_words, f_rest_scales):
    gain = f64(u)[:, None] + f64(v)[None, :] - f64(cost)
    new = np.maximum(f64(plan) + f64(step)[None, :] * gain, 0.0)
    hub = mxq(new[:, :H], 1, "e4m3") @ mxq(f64(f_hub), 0, "e4m3")
    rest = mxq(new[:, H:], 1, "e4m3") @ unpack4(f_rest_words, f_rest_scales)
    return hub + rest

@@ -1,0 +1,299 @@
+from contextlib import ExitStack
+
+import concourse.mybir as mybir
+from concourse.masks import make_identity
+
+M, H, L, D = 1024, 1024, 2048, 1024
+J = H + L
+FLOPS = 2 * M * J * D
+
+F32 = mybir.dt.float32
+BF16 = mybir.dt.bfloat16
+I32 = mybir.dt.int32
+U32 = mybir.dt.uint32
+U8 = mybir.dt.uint8
+FP8X4 = mybir.dt.float8_e4m3fn_x4
+FP4X4 = mybir.dt.float4_e2m1fn_x4
+ALU = mybir.AluOpType
+ACT = mybir.ActivationFunctionType
+
+P = 128
+PACK = 4
+K_PASS = P * PACK
+N_PASS = 512
+TILES = M // P
+PAIRS = TILES // 2
+PASSES = J // K_PASS
+HUB_PASSES = H // K_PASS
+REST_PASSES = L // K_PASS
+UNITS = PAIRS * PASSES
+PASS_ORDER = [2, 3, 4, 5, 0, 1]
+CHUNKS = [[1, 1, 1, 1, 1, 1], [1, 1, 2, 2], [4, 2], [4, 2]]
+FIRST_SLOTS = [3, 3, 4, 5, 6, 7]
+SECOND_SLOTS = [4, 5, 6, 7, 8, 8]
+
+
+def tile_transport_moment_step_s1_kernel(
+    tc, plan, cost, u, v, step, f_hub, f_rest_words, f_rest_scales, out
+):
+    nc = tc.nc
+    plan_rows = plan.rearrange("(p c) j -> p c j", c=TILES)
+    cost_rows = cost.rearrange("(p c) j -> p c j", c=TILES)
+    out_rows = out.rearrange("(p c) d -> p c d", c=TILES)
+    hub_rows = f_hub.rearrange("(g p t) d -> p g t d", p=P, t=PACK)
+
+    with ExitStack() as ctx:
+        keep = ctx.enter_context(tc.tile_pool(name="keep", bufs=1))
+        work = ctx.enter_context(tc.tile_pool(name="work", bufs=1))
+        psum = ctx.enter_context(tc.psum_pool(name="psum", bufs=1))
+        ctx.enter_context(tc.manual_schedule())
+
+        u_raw = keep.tile([P, TILES], BF16)
+        step_raw = keep.tile([P, PASSES, PACK], BF16)
+        v_raw = keep.tile([P, PASSES, PACK], BF16)
+        nc.scalar.dma_start(out=u_raw[:], in_=u.rearrange("(p c) -> p c", c=TILES))
+        nc.scalar.dma_start(out=step_raw[:], in_=step.rearrange("(g p t) -> p g t", p=P, t=PACK))
+        nc.scalar.dma_start(out=v_raw[:], in_=v.rearrange("(g p t) -> p g t", p=P, t=PACK))
+
+        ident = keep.tile([P, P], F32)
+        make_identity(nc, ident[:])
+
+        rest_scales = keep.tile([P, REST_PASSES, D], U8, align_bytes=64)
+        nc.vector.memset(rest_scales[:].bitcast(I32), 0)
+        warm_in = keep.tile([P, 1], F32)
+        warm_out = keep.tile([P, 1], F32)
+        nc.vector.memset(warm_in[:], 0.0)
+        nc.scalar.activation(out=warm_out[:], in_=warm_in[:], func=ACT.Identity, bias=warm_in[:], scale=-1.0)
+
+        u_col = keep.tile([P, TILES], F32)
+        step_col = keep.tile([P, PASSES, PACK], F32)
+        stepv_col = keep.tile([P, PASSES, PACK], F32)
+        nc.vector.tensor_copy(out=u_col[:], in_=u_raw[:])
+
+        cost_of, plan_of = {}, {}
+
+        def load_chunk(pair, first, count):
+            col0 = PASS_ORDER[first] * K_PASS
+            cols = slice(col0, col0 + count * K_PASS)
+            rows = slice(2 * pair, 2 * pair + 2)
+            name = "%d_%d" % (pair, first)
+            cost_sb = keep.tile([P, 2, count * K_PASS], BF16, name="cost" + name)
+            plan_sb = keep.tile([P, 2, count * K_PASS], BF16, name="plan" + name)
+            nc.sync.dma_start(out=cost_sb[:], in_=cost_rows[:, rows, cols])
+            nc.sync.dma_start(out=plan_sb[:], in_=plan_rows[:, rows, cols])
+            for j in range(count):
+                part = slice(j * K_PASS, (j + 1) * K_PASS)
+                cost_of[pair * PASSES + first + j] = cost_sb[:, :, part]
+                plan_of[pair * PASSES + first + j] = plan_sb[:, :, part]
+
+        hub_raw = {}
+
+        def load_hub(piece):
+            g, half = divmod(piece, 2)
+            raw = keep.tile([P, PACK, N_PASS], BF16, name="hub_raw%d" % piece)
+            nc.sync.dma_start(out=raw[:], in_=hub_rows[:, g, :, half * N_PASS : (half + 1) * N_PASS])
+            hub_raw[piece] = raw
+
+        rest_words = keep.tile([P, REST_PASSES, 2 * D], U8, align_bytes=64)
+
+        def load_rest_words(groups):
+            nc.sync.dma_start(
+                out=rest_words[:, groups, :].bitcast(I32),
+                in_=f_rest_words[groups].rearrange("g p n -> p g n").bitcast(I32),
+            )
+
+        def load_rest_scales():
+            for quad in range(4):
+                nc.sync.dma_start(
+                    out=rest_scales[32 * quad : 32 * quad + 4, :, :].bitcast(I32),
+                    in_=f_rest_scales[:, 4 * quad : 4 * quad + 4, :].rearrange("g r n -> r g n").bitcast(I32),
+                )
+
+        load_chunk(0, 0, 1)
+        load_hub(0)
+        load_chunk(0, 1, 1)
+        load_chunk(0, 2, 1)
+        load_rest_scales()
+        load_rest_words(slice(0, 2))
+        load_hub(1)
+        load_chunk(0, 3, 1)
+        load_chunk(0, 4, 1)
+        load_rest_words(slice(2, 4))
+        load_hub(2)
+        load_chunk(0, 5, 1)
+        load_hub(3)
+        for pair in range(1, PAIRS):
+            first = 0
+            for count in CHUNKS[pair]:
+                load_chunk(pair, first, count)
+                first += count
+
+        gain0, gain0_t, plan_t, scaled, summed, clipped, codes, scales = {}, {}, {}, {}, {}, {}, {}, {}
+
+        def subtract_cost(n, r, on_scalar):
+            if r == 0:
+                gain0[n] = work.tile([P, 2, PACK, P], F32, name="gain0", bufs=4)
+            src = cost_of[n][:, r, :].rearrange("p (m t) -> p t m", t=PACK)
+            tile_no = 2 * (n // PASSES) + r
+            u_here = u_col[:, tile_no : tile_no + 1]
+            if on_scalar:
+                nc.scalar.activation(out=gain0[n][:, r], in_=src, func=ACT.Identity, bias=u_here, scale=-1.0)
+            else:
+                nc.vector.tensor_scalar(
+                    out=gain0[n][:, r], in0=src, scalar1=u_here, scalar2=-1.0, op0=ALU.subtract, op1=ALU.mult
+                )
+
+        def transpose_unit(n):
+            gain0_t[n] = []
+            for h in range(2):
+                bank = psum.tile([P, 2, 2, P], F32, name="gain_bank", bufs=2)
+                for e in range(2):
+                    for r in range(2):
+                        nc.tensor.transpose(bank[:, e, r, :], gain0[n][:, r, 2 * h + e, :], ident[:])
+                gain0_t[n].append(bank)
+            bank = psum.tile([P, 2, 2, P], F32, name="plan_bank", bufs=2)
+            for h in range(2):
+                for r in range(2):
+                    words = plan_of[n][:, r, :].bitcast(F32)
+                    nc.tensor.transpose(bank[:, h, r, :], words[:, h : 2 * P : 2], ident[:])
+            plan_t[n] = bank
+
+        def scale_gain(n):
+            g = PASS_ORDER[n % PASSES]
+            scaled[n] = work.tile([P, 2, 2, 2 * P], F32, name="scaled", bufs=3)
+            for h in range(2):
+                for e in range(2):
+                    t = 2 * h + e
+                    nc.scalar.activation(
+                        out=scaled[n][:, h, e, :],
+                        in_=gain0_t[n][h][:, e].rearrange("p r m -> p (r m)"),
+                        func=ACT.Identity,
+                        bias=stepv_col[:, g, t : t + 1],
+                        scale=step_col[:, g, t : t + 1],
+                    )
+
+        def add_plan(n):
+            summed[n] = work.tile([P, 2, 2 * P, 2], BF16, name="summed", bufs=3)
+            nc.vector.tensor_tensor(
+                out=summed[n][:],
+                in0=scaled[n][:].rearrange("p h e i -> p h i e"),
+                in1=plan_t[n][:].rearrange("p h r m -> p (h r m)").bitcast(BF16).rearrange("p (h i e) -> p h i e", h=2, e=2),
+                op=ALU.add,
+            )
+
+        def clip(n):
+            clipped[n] = work.tile([P, 2 * P, 2, 2], BF16, name="clipped", bufs=3, align_bytes=64)
+            nc.vector.tensor_scalar_max(
+                out=clipped[n][:], in0=summed[n][:].rearrange("p h i e -> p i h e"), scalar1=0.0
+            )
+
+        def quantise(n):
+            codes[n] = work.tile([P, 2 * P], U32, name="codes", bufs=6, align_bytes=64)
+            scales[n] = work.tile([P, 2 * P], U8, name="scales", bufs=6, align_bytes=64)
+            nc.vector.quantize_mx(
+                out=codes[n][:].bitcast(FP8X4),
+                scales=scales[n][:],
+                in_=clipped[n][:].rearrange("p i h e -> p (i h e)"),
+            )
+
+        hub_grouped, hub_codes, hub_scales = {}, {}, {}
+
+        def interleave_hub(piece):
+            hub_grouped[piece] = work.tile([P, N_PASS, PACK], BF16, name="hub_grouped", bufs=2, align_bytes=64)
+            nc.vector.tensor_copy(out=hub_grouped[piece][:], in_=hub_raw[piece][:].rearrange("p t d -> p d t"))
+
+        def quantise_hub(piece):
+            hub_codes[piece] = keep.tile([P, N_PASS], U32, name="hub_codes%d" % piece, align_bytes=64)
+            hub_scales[piece] = keep.tile([P, N_PASS], U8, name="hub_scales%d" % piece, align_bytes=64)
+            nc.vector.quantize_mx(
+                out=hub_codes[piece][:].bitcast(FP8X4),
+                scales=hub_scales[piece][:],
+                in_=hub_grouped[piece][:].rearrange("p d t -> p (d t)"),
+            )
+
+        acc = {}
+
+        def multiply(n, r):
+            pair, j = divmod(n, PASSES)
+            g = PASS_ORDER[j]
+            rows = slice(r * P, (r + 1) * P)
+            for half in range(2):
+                if j == 0:
+                    acc[pair, r, half] = psum.tile([P, N_PASS], F32, name="acc%d%d" % (r, half))
+                if g < HUB_PASSES:
+                    rhs = hub_codes[2 * g + half][:].bitcast(FP8X4)
+                    rhs_scale = hub_scales[2 * g + half][:]
+                else:
+                    rhs = rest_words[:, g - HUB_PASSES, half * 2 * N_PASS : (half + 1) * 2 * N_PASS].bitcast(FP4X4)
+                    rhs_scale = rest_scales[:, g - HUB_PASSES, half * N_PASS : (half + 1) * N_PASS]
+                nc.tensor.matmul_mx(
+                    out=acc[pair, r, half][:],
+                    lhsT=codes[n][:, rows].bitcast(FP8X4),
+                    lhsT_scale=scales[n][:, rows],
+                    rhs=rhs,
+                    rhs_scale=rhs_scale,
+                    start=(j == 0),
+                    stop=(j == PASSES - 1),
+                )
+
+        def store_tile(pair, r):
+            result = work.tile([P, D], F32, name="result", bufs=3)
+            for half in range(2):
+                nc.scalar.copy(out=result[:, half * N_PASS : (half + 1) * N_PASS], in_=acc[pair, r, half][:])
+            nc.sync.dma_start(out=out_rows[:, 2 * pair + r, :], in_=result[:])
+
+        def store_last(pair, r):
+            for half in range(2):
+                piece = work.tile([P, N_PASS], F32, name="last%d%d" % (r, half))
+                if half == 0:
+                    nc.scalar.copy(out=piece[:], in_=acc[pair, r, half][:])
+                else:
+                    nc.vector.tensor_copy(out=piece[:], in_=acc[pair, r, half][:])
+                nc.sync.dma_start(
+                    out=out_rows[:, 2 * pair + r, half * N_PASS : (half + 1) * N_PASS], in_=piece[:]
+                )
+
+        slot_items = {}
+        for pair in range(PAIRS):
+            for j in range(PASSES):
+                for r, slots in enumerate((FIRST_SLOTS, SECOND_SLOTS)):
+                    slot = min(pair * PASSES + slots[j], UNITS)
+                    slot_items.setdefault(slot, []).append((pair * PASSES + j, r))
+        store_at = {}
+        for pair in range(PAIRS - 1):
+            store_at[pair * PASSES + FIRST_SLOTS[-1] + 1] = (pair, 0)
+            store_at[pair * PASSES + SECOND_SLOTS[-1] + 1] = (pair, 1)
+        hub_at = {0: 0, 2: 1, 4: 2, 5: 3}
+
+        subtract_cost(0, 0, False)
+        subtract_cost(0, 1, True)
+        nc.vector.tensor_copy(out=step_col[:], in_=step_raw[:])
+        nc.vector.tensor_tensor(out=stepv_col[:], in0=step_raw[:], in1=v_raw[:], op=ALU.mult)
+        interleave_hub(0)
+        subtract_cost(1, 0, False)
+        subtract_cost(1, 1, True)
+        quantise_hub(0)
+        for s in range(UNITS):
+            transpose_unit(s)
+            for n, r in sorted(slot_items.get(s, [])):
+                multiply(n, r)
+            scale_gain(s)
+            add_plan(s)
+            if s > 0:
+                quantise(s - 1)
+            hub_piece = hub_at.get(s) if s > 0 else None
+            if hub_piece is not None:
+                interleave_hub(hub_piece)
+            clip(s)
+            if hub_piece is not None:
+                quantise_hub(hub_piece)
+            if s + 2 < UNITS:
+                subtract_cost(s + 2, 0, hub_piece is not None)
+                subtract_cost(s + 2, 1, s not in store_at)
+            if s in store_at:
+                store_tile(*store_at[s])
+        quantise(UNITS - 1)
+        for n, r in sorted(slot_items[UNITS]):
+            multiply(n, r)
+        for r in range(2):
+            store_last(PAIRS - 1, r)

@@ -20,27 +20,71 @@ ACT = mybir.ActivationFunctionType
 P = 128
 PACK = 4
 K_PASS = P * PACK
-N_PASS = 512
+N_HALF = 512
 TILES = M // P
 PAIRS = TILES // 2
 PASSES = J // K_PASS
 HUB_PASSES = H // K_PASS
 REST_PASSES = L // K_PASS
-UNITS = PAIRS * PASSES
-PASS_ORDER = [2, 3, 4, 5, 0, 1]
-CHUNKS = [[1, 1, 1, 1, 1, 1], [1, 1, 2, 2], [4, 2], [4, 2]]
-FIRST_SLOTS = [3, 3, 4, 5, 6, 7]
-SECOND_SLOTS = [4, 5, 6, 7, 8, 8]
+PASS_ORDER = [0, 2, 3, 4, 5, 1]
+V_ROW = 8
+HUB_WIDTH = 256
+HUB_STEPS = [(-2, "vector"), (-1, "vector"), (-1, "vector"), (0, "scalar"),
+             (3, "vector"), (4, "scalar"), (5, "scalar"), (5, "scalar")]
+FIRST_SLOTS = ([3, 4, 5, 6, 6, 7], [3, 4, 5, 6, 8, 8])
+SLOTS = ([3, 3, 4, 5, 6, 7], [4, 5, 6, 7, 8, 8])
+LOADS = [
+    ("hub", 0, 0, 1),
+    ("cost", 0, 0, 1),
+    ("plan", 0, 0, 1),
+    ("cost", 0, 2, 1),
+    ("plan", 0, 2, 1),
+    ("cost", 0, 3, 2),
+    ("plan", 0, 3, 2),
+    ("cost", 0, 5, 1),
+    ("scales", 0, 0, 0),
+    ("cost", 0, 1, 1),
+    ("plan", 0, 5, 1),
+    ("hub", 0, 1, 1),
+    ("words", 0, 0, 2),
+    ("cost", 1, 0, 1),
+    ("plan", 0, 1, 1),
+    ("plan", 1, 0, 1),
+    ("cost", 1, 2, 2),
+    ("words", 0, 2, 2),
+    ("plan", 1, 2, 2),
+    ("cost", 1, 4, 2),
+    ("plan", 1, 4, 2),
+    ("cost", 1, 1, 1),
+    ("plan", 1, 1, 1),
+    ("cost", 2, 0, 3),
+    ("plan", 2, 0, 3),
+    ("cost", 2, 3, 3),
+    ("plan", 2, 3, 3),
+    ("cost", 3, 0, 6),
+    ("plan", 3, 0, 6),
+]
+EMPTY_AT = [(7, 0, 0, 0), (8, 0, 1, 0), (9, 0, 0, 1), (8, 0, 1, 1), (14, 1, 0, 0), (14, 1, 1, 0), (15, 1, 0, 1), (15, 1, 1, 1), (20, 2, 0, 0), (20, 2, 1, 0), (21, 2, 0, 1), (21, 2, 1, 1)]
+BOTH_ON_VECTOR = (0, 4, 5, 8, 14, 15, 20, 21)
+BOTH_ON_SCALAR = (1,)
 
 
 def tile_transport_moment_step_s1_kernel(
     tc, plan, cost, u, v, step, f_hub, f_rest_words, f_rest_scales, out
 ):
     nc = tc.nc
-    plan_rows = plan.rearrange("(p c) j -> p c j", c=TILES)
-    cost_rows = cost.rearrange("(p c) j -> p c j", c=TILES)
-    out_rows = out.rearrange("(p c) d -> p c d", c=TILES)
+    rows_of = {
+        "plan": plan.rearrange("(m c) j -> m c j", c=TILES),
+        "cost": cost.rearrange("(m c) j -> m c j", c=TILES),
+    }
+    out_rows = out.rearrange("(m c) d -> m c d", c=TILES)
     hub_rows = f_hub.rearrange("(g p t) d -> p g t d", p=P, t=PACK)
+
+    units = [(pair, g, (0, 1)) for pair in range(PAIRS) for g in PASS_ORDER]
+    whole_units = len(units)
+    last_pair, last_pass, both = units.pop()
+    units.extend((last_pair, last_pass, (r,)) for r in both)
+    steps = len(units)
 
     with ExitStack() as ctx:
         keep = ctx.enter_context(tc.tile_pool(name="keep", bufs=1))
@@ -48,252 +92,250 @@ def tile_transport_moment_step_s1_kernel(
         psum = ctx.enter_context(tc.psum_pool(name="psum", bufs=1))
         ctx.enter_context(tc.manual_schedule())
 
-        u_raw = keep.tile([P, TILES], BF16)
-        step_raw = keep.tile([P, PASSES, PACK], BF16)
-        v_raw = keep.tile([P, PASSES, PACK], BF16)
-        nc.scalar.dma_start(out=u_raw[:], in_=u.rearrange("(p c) -> p c", c=TILES))
-        nc.scalar.dma_start(out=step_raw[:], in_=step.rearrange("(g p t) -> p g t", p=P, t=PACK))
-        nc.scalar.dma_start(out=v_raw[:], in_=v.rearrange("(g p t) -> p g t", p=P, t=PACK))
+        vectors = keep.tile([P, K_PASS], BF16)
+        nc.vector.memset(vectors[:].bitcast(I32), 0)
+        u_col = keep.tile([P, TILES], BF16)
+        nc.scalar.dma_start(out=u_col[:], in_=u.rearrange("(m c) -> m c", c=TILES))
+        for lo, hi in ((0, 4), (4, PASSES)):
+            nc.scalar.dma_start(out=vectors[lo:hi, :], in_=step.rearrange("(g k) -> g k", k=K_PASS)[lo:hi, :])
+            nc.scalar.dma_start(
+                out=vectors[V_ROW + lo : V_ROW + hi, :], in_=v.rearrange("(g k) -> g k", k=K_PASS)[lo:hi, :]
+            )
 
         ident = keep.tile([P, P], F32)
         make_identity(nc, ident[:])
 
         rest_scales = keep.tile([P, REST_PASSES, D], U8, align_bytes=64)
-        nc.vector.memset(rest_scales[:].bitcast(I32), 0)
         warm_in = keep.tile([P, 1], F32)
         warm_out = keep.tile([P, 1], F32)
         nc.vector.memset(warm_in[:], 0.0)
+        nc.vector.memset(rest_scales[:].bitcast(I32), 0)
         nc.scalar.activation(out=warm_out[:], in_=warm_in[:], func=ACT.Identity, bias=warm_in[:], scale=-1.0)
 
-        u_col = keep.tile([P, TILES], F32)
-        step_col = keep.tile([P, PASSES, PACK], F32)
-        stepv_col = keep.tile([P, PASSES, PACK], F32)
-        nc.vector.tensor_copy(out=u_col[:], in_=u_raw[:])
-
-        cost_of, plan_of = {}, {}
-
-        def load_chunk(pair, first, count):
-            col0 = PASS_ORDER[first] * K_PASS
-            cols = slice(col0, col0 + count * K_PASS)
-            rows = slice(2 * pair, 2 * pair + 2)
-            name = "%d_%d" % (pair, first)
-            cost_sb = keep.tile([P, 2, count * K_PASS], BF16, name="cost" + name)
-            plan_sb = keep.tile([P, 2, count * K_PASS], BF16, name="plan" + name)
-            nc.sync.dma_start(out=cost_sb[:], in_=cost_rows[:, rows, cols])
-            nc.sync.dma_start(out=plan_sb[:], in_=plan_rows[:, rows, cols])
-            for j in range(count):
-                part = slice(j * K_PASS, (j + 1) * K_PASS)
-                cost_of[pair * PASSES + first + j] = cost_sb[:, :, part]
-                plan_of[pair * PASSES + first + j] = plan_sb[:, :, part]
-
-        hub_raw = {}
-
-        def load_hub(piece):
-            g, half = divmod(piece, 2)
-            raw = keep.tile([P, PACK, N_PASS], BF16, name="hub_raw%d" % piece)
-            nc.sync.dma_start(out=raw[:], in_=hub_rows[:, g, :, half * N_PASS : (half + 1) * N_PASS])
-            hub_raw[piece] = raw
-
+        hub_raw = keep.tile([P, HUB_PASSES, PACK, D], BF16)
         rest_words = keep.tile([P, REST_PASSES, 2 * D], U8, align_bytes=64)
+        loaded = {}
+        for pair in range(PAIRS):
+            for kind in ("cost", "plan"):
+                loaded[kind, pair] = keep.tile([P, 2, J], BF16, name="%s%d" % (kind, pair))
 
-        def load_rest_words(groups):
-            nc.sync.dma_start(
-                out=rest_words[:, groups, :].bitcast(I32),
-                in_=f_rest_words[groups].rearrange("g p n -> p g n").bitcast(I32),
-            )
-
-        def load_rest_scales():
-            for quad in range(4):
+        for kind, pair, first, count in LOADS:
+            if kind == "hub":
+                nc.sync.dma_start(out=hub_raw[:, first], in_=hub_rows[:, first])
+            elif kind == "words":
+                groups = slice(first, first + count)
                 nc.sync.dma_start(
-                    out=rest_scales[32 * quad : 32 * quad + 4, :, :].bitcast(I32),
-                    in_=f_rest_scales[:, 4 * quad : 4 * quad + 4, :].rearrange("g r n -> r g n").bitcast(I32),
+                    out=rest_words[:, groups, :].bitcast(I32),
+                    in_=f_rest_words[groups].rearrange("g p n -> p g n").bitcast(I32),
                 )
-
-        load_chunk(0, 0, 1)
-        load_hub(0)
-        load_chunk(0, 1, 1)
-        load_chunk(0, 2, 1)
-        load_rest_scales()
-        load_rest_words(slice(0, 2))
-        load_hub(1)
-        load_chunk(0, 3, 1)
-        load_chunk(0, 4, 1)
-        load_rest_words(slice(2, 4))
-        load_hub(2)
-        load_chunk(0, 5, 1)
-        load_hub(3)
-        for pair in range(1, PAIRS):
-            first = 0
-            for count in CHUNKS[pair]:
-                load_chunk(pair, first, count)
-                first += count
-
-        gain0, gain0_t, plan_t, scaled, summed, clipped, codes, scales = {}, {}, {}, {}, {}, {}, {}, {}
-
-        def subtract_cost(n, r, on_scalar):
-            if r == 0:
-                gain0[n] = work.tile([P, 2, PACK, P], F32, name="gain0", bufs=4)
-            src = cost_of[n][:, r, :].rearrange("p (m t) -> p t m", t=PACK)
-            tile_no = 2 * (n // PASSES) + r
-            u_here = u_col[:, tile_no : tile_no + 1]
-            if on_scalar:
-                nc.scalar.activation(out=gain0[n][:, r], in_=src, func=ACT.Identity, bias=u_here, scale=-1.0)
-            else:
-                nc.vector.tensor_scalar(
-                    out=gain0[n][:, r], in0=src, scalar1=u_here, scalar2=-1.0, op0=ALU.subtract, op1=ALU.mult
-                )
-
-        def transpose_unit(n):
-            gain0_t[n] = []
-            for h in range(2):
-                bank = psum.tile([P, 2, 2, P], F32, name="gain_bank", bufs=2)
-                for e in range(2):
-                    for r in range(2):
-                        nc.tensor.transpose(bank[:, e, r, :], gain0[n][:, r, 2 * h + e, :], ident[:])
-                gain0_t[n].append(bank)
-            bank = psum.tile([P, 2, 2, P], F32, name="plan_bank", bufs=2)
-            for h in range(2):
-                for r in range(2):
-                    words = plan_of[n][:, r, :].bitcast(F32)
-                    nc.tensor.transpose(bank[:, h, r, :], words[:, h : 2 * P : 2], ident[:])
-            plan_t[n] = bank
-
-        def scale_gain(n):
-            g = PASS_ORDER[n % PASSES]
-            scaled[n] = work.tile([P, 2, 2, 2 * P], F32, name="scaled", bufs=3)
-            for h in range(2):
-                for e in range(2):
-                    t = 2 * h + e
-                    nc.scalar.activation(
-                        out=scaled[n][:, h, e, :],
-                        in_=gain0_t[n][h][:, e].rearrange("p r m -> p (r m)"),
-                        func=ACT.Identity,
-                        bias=stepv_col[:, g, t : t + 1],
-                        scale=step_col[:, g, t : t + 1],
+            elif kind == "scales":
+                for quad in range(4):
+                    nc.sync.dma_start(
+                        out=rest_scales[32 * quad : 32 * quad + 4, :, :].bitcast(I32),
+                        in_=f_rest_scales[:, 4 * quad : 4 * quad + 4, :].rearrange("g r n -> r g n").bitcast(I32),
                     )
+            else:
+                cols = slice(first * K_PASS, (first + count) * K_PASS)
+                nc.sync.dma_start(
+                    out=loaded[kind, pair][:, :, cols], in_=rows_of[kind][:, 2 * pair : 2 * pair + 2, cols]
+                )
 
-        def add_plan(n):
-            summed[n] = work.tile([P, 2, 2 * P, 2], BF16, name="summed", bufs=3)
+        step_col = keep.tile([P, PASSES, 2, 2], F32)
+        stepv_col = keep.tile([P, PASSES, 2, 2], F32)
+        turned_bank = psum.tile([P, 2, 2, P], F32, name="plan_bank", bufs=2)
+        for h in range(2):
+            nc.tensor.transpose(turned_bank[:, h, 0, :], vectors[:].bitcast(F32)[:, h : 2 * P : 2], ident[:])
+        turned = turned_bank[:, :, 0, :].bitcast(BF16).rearrange("p h (g e) -> p g h e", e=2)
+        nc.vector.tensor_copy(out=step_col[:], in_=turned[:, 0:PASSES])
+        nc.vector.tensor_tensor(out=stepv_col[:], in0=step_col[:], in1=turned[:, V_ROW : V_ROW + PASSES], op=ALU.mult)
+
+        slack, slack_t, plan_t, scaled, summed, clipped, codes, scales = {}, {}, {}, {}, {}, {}, {}, {}
+
+        def subtract(n, r, engine):
+            pair, g, rs = units[n]
+            if (pair, g) not in slack:
+                slack[pair, g] = work.tile([P, 2, PACK, P], F32, name="slack", bufs=4)
+            dst = slack[pair, g][:, r]
+            src = loaded["cost", pair][:, r, g * K_PASS : (g + 1) * K_PASS].rearrange("m (p t) -> m t p", t=PACK)
+            u_here = u_col[:, 2 * pair + r : 2 * pair + r + 1]
+            if engine == "scalar":
+                nc.scalar.activation(out=dst, in_=src, func=ACT.Identity, bias=u_here, scale=-1.0)
+            else:
+                nc.vector.tensor_scalar(out=dst, in0=src, scalar1=-1.0, scalar2=u_here, op0=ALU.mult, op1=ALU.add)
+
+        def transpose(n):
+            pair, g, rs = units[n]
+            per_bank = PACK // len(rs)
+            slack_t[n] = []
+            for t in range(PACK):
+                if t % per_bank == 0:
+                    bank = psum.tile([P, per_bank, len(rs) * P], F32, name="slack_bank", bufs=2)
+                for place, r in enumerate(rs):
+                    nc.tensor.transpose(
+                        bank[:, t % per_bank, place * P : (place + 1) * P], slack[pair, g][:, r, t, :], ident[:]
+                    )
+                slack_t[n].append(bank[:, t % per_bank, :])
+            plan_t[n] = psum.tile([P, 2, len(rs) * P], F32, name="plan_bank", bufs=2)
+            for h in range(2):
+                for place, r in enumerate(rs):
+                    words = loaded["plan", pair][:, r, g * K_PASS : (g + 1) * K_PASS].bitcast(F32)
+                    nc.tensor.transpose(plan_t[n][:, h, place * P : (place + 1) * P], words[:, h : 2 * P : 2], ident[:])
+
+        def scale(n):
+            pair, g, rs = units[n]
+            scaled[n] = work.tile([P, 2, 2, len(rs) * P], F32, name="scaled", bufs=3)
+            for t in range(PACK):
+                h, e = divmod(t, 2)
+                nc.scalar.activation(
+                    out=scaled[n][:, h, e, :],
+                    in_=slack_t[n][t],
+                    func=ACT.Identity,
+                    bias=stepv_col[:, g, h, e : e + 1],
+                    scale=step_col[:, g, h, e : e + 1],
+                )
+
+        def add(n):
+            width = len(units[n][2]) * P
+            summed[n] = work.tile([P, 2, width, 2], BF16, name="summed", bufs=3)
             nc.vector.tensor_tensor(
                 out=summed[n][:],
                 in0=scaled[n][:].rearrange("p h e i -> p h i e"),
-                in1=plan_t[n][:].rearrange("p h r m -> p (h r m)").bitcast(BF16).rearrange("p (h i e) -> p h i e", h=2, e=2),
+                in1=plan_t[n][:].bitcast(BF16).rearrange("p h (i e) -> p h i e", e=2),
                 op=ALU.add,
             )
 
         def clip(n):
-            clipped[n] = work.tile([P, 2 * P, 2, 2], BF16, name="clipped", bufs=3, align_bytes=64)
+            width = len(units[n][2]) * P
+            clipped[n] = work.tile([P, width, 2, 2], BF16, name="clipped", bufs=3, align_bytes=64)
             nc.vector.tensor_scalar_max(
                 out=clipped[n][:], in0=summed[n][:].rearrange("p h i e -> p i h e"), scalar1=0.0
             )
 
         def quantise(n):
-            codes[n] = work.tile([P, 2 * P], U32, name="codes", bufs=6, align_bytes=64)
-            scales[n] = work.tile([P, 2 * P], U8, name="scales", bufs=6, align_bytes=64)
+            width = len(units[n][2]) * P
+            codes[n] = work.tile([P, width], U32, name="codes", bufs=8, align_bytes=64)
+            scales[n] = work.tile([P, width], U8, name="scales", bufs=8, align_bytes=64)
             nc.vector.quantize_mx(
                 out=codes[n][:].bitcast(FP8X4),
                 scales=scales[n][:],
                 in_=clipped[n][:].rearrange("p i h e -> p (i h e)"),
             )
 
-        hub_grouped, hub_codes, hub_scales = {}, {}, {}
+        hub_grouped = {}
+        hub_codes = keep.tile([P, HUB_PASSES, D], U32, align_bytes=64)
+        hub_scales = keep.tile([P, HUB_PASSES, D], U8, align_bytes=64)
 
-        def interleave_hub(piece):
-            hub_grouped[piece] = work.tile([P, N_PASS, PACK], BF16, name="hub_grouped", bufs=2, align_bytes=64)
-            nc.vector.tensor_copy(out=hub_grouped[piece][:], in_=hub_raw[piece][:].rearrange("p t d -> p d t"))
+        def hub_pieces(at):
+            for piece, (piece_step, engine) in enumerate(HUB_STEPS):
+                if piece_step == at:
+                    g, part = divmod(piece, D // HUB_WIDTH)
+                    cols = slice(part * HUB_WIDTH, (part + 1) * HUB_WIDTH)
+                    hub_todo.append((piece, g, cols, engine))
 
-        def quantise_hub(piece):
-            hub_codes[piece] = keep.tile([P, N_PASS], U32, name="hub_codes%d" % piece, align_bytes=64)
-            hub_scales[piece] = keep.tile([P, N_PASS], U8, name="hub_scales%d" % piece, align_bytes=64)
-            nc.vector.quantize_mx(
-                out=hub_codes[piece][:].bitcast(FP8X4),
-                scales=hub_scales[piece][:],
-                in_=hub_grouped[piece][:].rearrange("p d t -> p (d t)"),
-            )
+        hub_todo = []
+
+        def interleave_hub(at):
+            hub_todo.clear()
+            hub_pieces(at)
+            for piece, g, cols, engine in hub_todo:
+                hub_grouped[piece] = work.tile([P, HUB_WIDTH, PACK], BF16, name="hub_grouped", bufs=4, align_bytes=64)
+                src = hub_raw[:, g, :, cols].rearrange("p t d -> p d t")
+                if engine == "scalar":
+                    nc.scalar.copy(out=hub_grouped[piece][:], in_=src)
+                else:
+                    nc.vector.tensor_copy(out=hub_grouped[piece][:], in_=src)
+
+        def quantise_hub(at):
+            hub_todo.clear()
+            hub_pieces(at)
+            for piece, g, cols, engine in hub_todo:
+                nc.vector.quantize_mx(
+                    out=hub_codes[:, g, cols].bitcast(FP8X4),
+                    scales=hub_scales[:, g, cols],
+                    in_=hub_grouped[piece][:].rearrange("p d t -> p (d t)"),
+                )
 
         acc = {}
 
-        def multiply(n, r):
-            pair, j = divmod(n, PASSES)
-            g = PASS_ORDER[j]
-            rows = slice(r * P, (r + 1) * P)
-            for half in range(2):
-                if j == 0:
-                    acc[pair, r, half] = psum.tile([P, N_PASS], F32, name="acc%d%d" % (r, half))
-                if g < HUB_PASSES:
-                    rhs = hub_codes[2 * g + half][:].bitcast(FP8X4)
-                    rhs_scale = hub_scales[2 * g + half][:]
-                else:
-                    rhs = rest_words[:, g - HUB_PASSES, half * 2 * N_PASS : (half + 1) * 2 * N_PASS].bitcast(FP4X4)
-                    rhs_scale = rest_scales[:, g - HUB_PASSES, half * N_PASS : (half + 1) * N_PASS]
-                nc.tensor.matmul_mx(
-                    out=acc[pair, r, half][:],
-                    lhsT=codes[n][:, rows].bitcast(FP8X4),
-                    lhsT_scale=scales[n][:, rows],
-                    rhs=rhs,
-                    rhs_scale=rhs_scale,
-                    start=(j == 0),
-                    stop=(j == PASSES - 1),
-                )
+        def multiply(n, r, half):
+            pair, g, rs = units[n]
+            rows = slice(rs.index(r) * P, (rs.index(r) + 1) * P)
+            cols = slice(half * N_HALF, (half + 1) * N_HALF)
+            if g == PASS_ORDER[0]:
+                acc[pair, r, half] = psum.tile([P, N_HALF], F32, name="acc%d%d" % (r, half))
+            if g < HUB_PASSES:
+                rhs = hub_codes[:, g, cols].bitcast(FP8X4)
+                rhs_scale = hub_scales[:, g, cols]
+            else:
+                rhs = rest_words[:, g - HUB_PASSES, half * 2 * N_HALF : (half + 1) * 2 * N_HALF].bitcast(FP4X4)
+                rhs_scale = rest_scales[:, g - HUB_PASSES, cols]
+            nc.tensor.matmul_mx(
+                out=acc[pair, r, half][:],
+                lhsT=codes[n][:, rows].bitcast(FP8X4),
+                lhsT_scale=scales[n][:, rows],
+                rhs=rhs,
+                rhs_scale=rhs_scale,
+                start=(g == PASS_ORDER[0]),
+                stop=(g == PASS_ORDER[-1]),
+            )
 
-        def store_tile(pair, r):
-            result = work.tile([P, D], F32, name="result", bufs=3)
-            for half in range(2):
-                nc.scalar.copy(out=result[:, half * N_PASS : (half + 1) * N_PASS], in_=acc[pair, r, half][:])
-            nc.sync.dma_start(out=out_rows[:, 2 * pair + r, :], in_=result[:])
+        def empty(pair, r, half, engine):
+            result = work.tile([P, N_HALF], F32, name="result", bufs=6)
+            if engine == "scalar":
+                nc.scalar.copy(out=result[:], in_=acc[pair, r, half][:])
+            else:
+                nc.vector.tensor_copy(out=result[:], in_=acc[pair, r, half][:])
+            nc.sync.dma_start(out=out_rows[:, 2 * pair + r, half * N_HALF : (half + 1) * N_HALF], in_=result[:])
 
-        def store_last(pair, r):
-            for half in range(2):
-                piece = work.tile([P, N_PASS], F32, name="last%d%d" % (r, half))
-                if half == 0:
-                    nc.scalar.copy(out=piece[:], in_=acc[pair, r, half][:])
-                else:
-                    nc.vector.tensor_copy(out=piece[:], in_=acc[pair, r, half][:])
-                nc.sync.dma_start(
-                    out=out_rows[:, 2 * pair + r, half * N_PASS : (half + 1) * N_PASS], in_=piece[:]
-                )
+        products = {}
+        for n, (pair, g, rs) in enumerate(units):
+            for r in rs:
+                for half in range(2):
+                    slot = pair * PASSES + (SLOTS if pair else FIRST_SLOTS)[half][PASS_ORDER.index(g)]
+                    if slot == steps - 2:
+                        slot = steps - 1
+                    products.setdefault(min(slot, steps), []).append((n, r, half))
 
-        slot_items = {}
-        for pair in range(PAIRS):
-            for j in range(PASSES):
-                for r, slots in enumerate((FIRST_SLOTS, SECOND_SLOTS)):
-                    slot = min(pair * PASSES + slots[j], UNITS)
-                    slot_items.setdefault(slot, []).append((pair * PASSES + j, r))
-        store_at = {}
-        for pair in range(PAIRS - 1):
-            store_at[pair * PASSES + FIRST_SLOTS[-1] + 1] = (pair, 0)
-            store_at[pair * PASSES + SECOND_SLOTS[-1] + 1] = (pair, 1)
-        hub_at = {0: 0, 2: 1, 4: 2, 5: 3}
+        def engines_at(s):
+            if s in BOTH_ON_VECTOR:
+                return "vector", "vector"
+            if s in BOTH_ON_SCALAR:
+                return "scalar", "scalar"
+            return "vector", "scalar"
 
-        subtract_cost(0, 0, False)
-        subtract_cost(0, 1, True)
-        nc.vector.tensor_copy(out=step_col[:], in_=step_raw[:])
-        nc.vector.tensor_tensor(out=stepv_col[:], in0=step_raw[:], in1=v_raw[:], op=ALU.mult)
-        interleave_hub(0)
-        subtract_cost(1, 0, False)
-        subtract_cost(1, 1, True)
-        quantise_hub(0)
-        for s in range(UNITS):
-            transpose_unit(s)
-            for n, r in sorted(slot_items.get(s, [])):
-                multiply(n, r)
-            scale_gain(s)
-            add_plan(s)
-            if s > 0:
+        def quantise_later(s):
+            return s + 2 < whole_units and engines_at(s)[1] == "scalar"
+
+        interleave_hub(-2)
+        subtract(0, 0, "vector")
+        subtract(0, 1, "scalar")
+        quantise_hub(-2)
+        interleave_hub(-1)
+        subtract(1, 0, "vector")
+        subtract(1, 1, "vector")
+        for s in range(steps):
+            transpose(s)
+            for item in sorted(products.get(s, [])):
+                multiply(*item)
+            scale(s)
+            add(s)
+            if s > 0 and quantise_later(s - 1):
                 quantise(s - 1)
-            hub_piece = hub_at.get(s) if s > 0 else None
-            if hub_piece is not None:
-                interleave_hub(hub_piece)
+            for at, pair, r, half in EMPTY_AT:
+                if at == s:
+                    empty(pair, r, half, "scalar")
+            if s + 2 < whole_units:
+                subtract(s + 2, 0, engines_at(s)[0])
             clip(s)
-            if hub_piece is not None:
-                quantise_hub(hub_piece)
-            if s + 2 < UNITS:
-                subtract_cost(s + 2, 0, hub_piece is not None)
-                subtract_cost(s + 2, 1, s not in store_at)
-            if s in store_at:
-                store_tile(*store_at[s])
-        quantise(UNITS - 1)
-        for n, r in sorted(slot_items[UNITS]):
-            multiply(n, r)
+            if s + 2 < whole_units:
+                subtract(s + 2, 1, engines_at(s)[1])
+            quantise_hub(s - 1)
+            if not quantise_later(s):
+                quantise(s)
+            interleave_hub(s)
         for r in range(2):
-            store_last(PAIRS - 1, r)
+            for half in range(2):
+                for item in sorted(products[steps]):
+                    if item[1:] == (r, half):
+                        multiply(*item)
+                empty(PAIRS - 1, r, half, "vector" if half else "scalar")

@@ -29,8 +29,7 @@ REST_PASSES = L // K_PASS
 PASS_ORDER = [0, 2, 3, 4, 5, 1]
 V_ROW = 8
 HUB_WIDTH = 256
-HUB_STEPS = [(-2, "vector"), (-1, "vector"), (-1, "vector"), (0, "scalar"),
-             (3, "vector"), (4, "scalar"), (5, "scalar"), (5, "scalar")]
+HUB_STEPS = [(-2, "vector"), (-1, "vector"), (-1, "vector"), (0, "scalar"), (3, "scalar"), (4, "scalar"), (5, "scalar"), (5, "vector")]
 FIRST_SLOTS = ([3, 4, 5, 6, 6, 7], [3, 4, 5, 6, 8, 8])
 SLOTS = ([3, 3, 4, 5, 6, 7], [4, 5, 6, 7, 8, 8])
 LOADS = [
@@ -65,8 +64,10 @@ LOADS = [
     ("plan", 3, 0, 6),
 ]
 EMPTY_AT = [(7, 0, 0, 0), (8, 0, 1, 0), (9, 0, 0, 1), (8, 0, 1, 1), (14, 1, 0, 0), (14, 1, 1, 0), (15, 1, 0, 1), (15, 1, 1, 1), (20, 2, 0, 0), (20, 2, 1, 0), (21, 2, 0, 1), (21, 2, 1, 1)]
-BOTH_ON_VECTOR = (0, 4, 5, 8, 14, 15, 20, 21)
-BOTH_ON_SCALAR = (1,)
+SECOND_ON_VECTOR = (0, 3, 4, 5, 8, 9, 14, 15, 20, 21)
+POOL_FROM = 3
+SORT_FROM = 8
+LAST_LATE = 21
 
 
 def tile_transport_moment_step_s1_kernel(
@@ -115,9 +116,6 @@ def tile_transport_moment_step_s1_kernel(
         hub_raw = keep.tile([P, HUB_PASSES, PACK, D], BF16)
         rest_words = keep.tile([P, REST_PASSES, 2 * D], U8, align_bytes=64)
         loaded = {}
-        for pair in range(PAIRS):
-            for kind in ("cost", "plan"):
-                loaded[kind, pair] = keep.tile([P, 2, J], BF16, name="%s%d" % (kind, pair))
 
         for kind, pair, first, count in LOADS:
             if kind == "hub":
@@ -136,9 +134,10 @@ def tile_transport_moment_step_s1_kernel(
                     )
             else:
                 cols = slice(first * K_PASS, (first + count) * K_PASS)
-                nc.sync.dma_start(
-                    out=loaded[kind, pair][:, :, cols], in_=rows_of[kind][:, 2 * pair : 2 * pair + 2, cols]
-                )
+                chunk = keep.tile([P, 2, count * K_PASS], BF16, name="%s%d_%d" % (kind, pair, first))
+                nc.sync.dma_start(out=chunk[:], in_=rows_of[kind][:, 2 * pair : 2 * pair + 2, cols])
+                for g in range(first, first + count):
+                    loaded[kind, pair, g] = chunk[:, :, (g - first) * K_PASS : (g - first + 1) * K_PASS]
 
         step_col = keep.tile([P, PASSES, 2, 2], F32)
         stepv_col = keep.tile([P, PASSES, 2, 2], F32)
@@ -156,12 +155,28 @@ def tile_transport_moment_step_s1_kernel(
             if (pair, g) not in slack:
                 slack[pair, g] = work.tile([P, 2, PACK, P], F32, name="slack", bufs=4)
             dst = slack[pair, g][:, r]
-            src = loaded["cost", pair][:, r, g * K_PASS : (g + 1) * K_PASS].rearrange("m (p t) -> m t p", t=PACK)
+            src = loaded["cost", pair, g][:, r, :].rearrange("m (p t) -> m t p", t=PACK)
             u_here = u_col[:, 2 * pair + r : 2 * pair + r + 1]
             if engine == "scalar":
                 nc.scalar.activation(out=dst, in_=src, func=ACT.Identity, bias=u_here, scale=-1.0)
-            else:
+            elif engine == "vector":
                 nc.vector.tensor_scalar(out=dst, in0=src, scalar1=-1.0, scalar2=u_here, op0=ALU.mult, op1=ALU.add)
+            else:
+                nc.gpsimd.tensor_scalar(out=dst, in0=src, scalar1=-1.0, scalar2=gate[n][:], op0=ALU.mult, op1=ALU.add)
+
+        gate, paired = {}, {}
+
+        def open_gate(n):
+            gate[n] = work.tile([P, 1], F32, name="gate", bufs=4)
+            tile_no = 2 * units[n][0]
+            nc.vector.tensor_copy(out=gate[n][:], in_=u_col[:, tile_no : tile_no + 1])
+
+        def sort_words(n):
+            pair, g, rs = units[n]
+            paired[pair, g] = work.tile([P, 2, 2, P], F32, name="paired", bufs=3)
+            nc.vector.tensor_copy(
+                out=paired[pair, g][:], in_=loaded["plan", pair, g].bitcast(F32).rearrange("m r (p h) -> m r h p", h=2)
+            )
 
         def transpose(n):
             pair, g, rs = units[n]
@@ -178,8 +193,11 @@ def tile_transport_moment_step_s1_kernel(
             plan_t[n] = psum.tile([P, 2, len(rs) * P], F32, name="plan_bank", bufs=2)
             for h in range(2):
                 for place, r in enumerate(rs):
-                    words = loaded["plan", pair][:, r, g * K_PASS : (g + 1) * K_PASS].bitcast(F32)
-                    nc.tensor.transpose(plan_t[n][:, h, place * P : (place + 1) * P], words[:, h : 2 * P : 2], ident[:])
+                    if (pair, g) in paired:
+                        words = paired[pair, g][:, r, h, :]
+                    else:
+                        words = loaded["plan", pair, g][:, r, :].bitcast(F32)[:, h : 2 * P : 2]
+                    nc.tensor.transpose(plan_t[n][:, h, place * P : (place + 1) * P], words, ident[:])
 
         def scale(n):
             pair, g, rs = units[n]
@@ -234,10 +252,12 @@ def tile_transport_moment_step_s1_kernel(
 
         hub_todo = []
 
-        def interleave_hub(at):
+        def interleave_hub(at, only=None):
             hub_todo.clear()
             hub_pieces(at)
             for piece, g, cols, engine in hub_todo:
+                if only and engine != only:
+                    continue
                 hub_grouped[piece] = work.tile([P, HUB_WIDTH, PACK], BF16, name="hub_grouped", bufs=4, align_bytes=64)
                 src = hub_raw[:, g, :, cols].rearrange("p t d -> p d t")
                 if engine == "scalar":
@@ -296,16 +316,6 @@ def tile_transport_moment_step_s1_kernel(
                         slot = steps - 1
                     products.setdefault(min(slot, steps), []).append((n, r, half))
 
-        def engines_at(s):
-            if s in BOTH_ON_VECTOR:
-                return "vector", "vector"
-            if s in BOTH_ON_SCALAR:
-                return "scalar", "scalar"
-            return "vector", "scalar"
-
-        def quantise_later(s):
-            return s + 2 < whole_units and engines_at(s)[1] == "scalar"
-
         interleave_hub(-2)
         subtract(0, 0, "vector")
         subtract(0, 1, "scalar")
@@ -314,25 +324,33 @@ def tile_transport_moment_step_s1_kernel(
         subtract(1, 0, "vector")
         subtract(1, 1, "vector")
         for s in range(steps):
+            ahead = s + 2 if s + 2 < whole_units else None
             transpose(s)
             for item in sorted(products.get(s, [])):
                 multiply(*item)
             scale(s)
             add(s)
-            if s > 0 and quantise_later(s - 1):
+            if 0 < s <= LAST_LATE + 1:
                 quantise(s - 1)
             for at, pair, r, half in EMPTY_AT:
                 if at == s:
                     empty(pair, r, half, "scalar")
-            if s + 2 < whole_units:
-                subtract(s + 2, 0, engines_at(s)[0])
-            clip(s)
-            if s + 2 < whole_units:
-                subtract(s + 2, 1, engines_at(s)[1])
+            if ahead and ahead not in gate:
+                subtract(ahead, 0, "vector")
+            if ahead:
+                subtract(ahead, 1, "vector" if s in SECOND_ON_VECTOR else "scalar")
+            if ahead and ahead >= SORT_FROM:
+                sort_words(ahead)
             quantise_hub(s - 1)
-            if not quantise_later(s):
+            for piece_engine in ("vector", "scalar"):
+                interleave_hub(s, piece_engine)
+            if POOL_FROM <= s + 3 < whole_units:
+                open_gate(s + 3)
+            clip(s)
+            if POOL_FROM <= s + 3 < whole_units:
+                subtract(s + 3, 0, "gpsimd")
+            if s > LAST_LATE:
                 quantise(s)
-            interleave_hub(s)
         for r in range(2):
             for half in range(2):
                 for item in sorted(products[steps]):

@@ -26,48 +26,30 @@ PAIRS = TILES // 2
 PASSES = J // K_PASS
 HUB_PASSES = H // K_PASS
 REST_PASSES = L // K_PASS
-PASS_ORDER = [0, 2, 3, 4, 5, 1]
 V_ROW = 8
+
+PASS_ORDER = [0, 2, 3, 4, 5, 1]
+
 HUB_WIDTH = 256
-HUB_STEPS = [(-2, "vector"), (-1, "vector"), (-1, "vector"), (0, "scalar"), (3, "scalar"), (4, "scalar"), (5, "scalar"), (5, "vector")]
-FIRST_SLOTS = ([3, 4, 5, 6, 6, 7], [3, 4, 5, 6, 8, 8])
+HUB_STEPS = [(-1, "vector")] * 3 + [(0, "scalar")] + [(s, "scalar") for s in (3, 4, 5, 6)]
+
 SLOTS = ([3, 3, 4, 5, 6, 7], [4, 5, 6, 7, 8, 8])
+FIRST_SLOTS = ([3, 4, 5, 6, 7, 7], [4, 5, 6, 7, 8, 8])
+
 LOADS = [
-    ("hub", 0, 0, 1),
-    ("cost", 0, 0, 1),
-    ("plan", 0, 0, 1),
-    ("cost", 0, 2, 1),
-    ("plan", 0, 2, 1),
-    ("cost", 0, 3, 2),
-    ("plan", 0, 3, 2),
-    ("cost", 0, 5, 1),
-    ("scales", 0, 0, 0),
-    ("cost", 0, 1, 1),
-    ("plan", 0, 5, 1),
-    ("hub", 0, 1, 1),
-    ("words", 0, 0, 2),
-    ("cost", 1, 0, 1),
-    ("plan", 0, 1, 1),
-    ("plan", 1, 0, 1),
-    ("cost", 1, 2, 2),
-    ("words", 0, 2, 2),
-    ("plan", 1, 2, 2),
-    ("cost", 1, 4, 2),
-    ("plan", 1, 4, 2),
-    ("cost", 1, 1, 1),
-    ("plan", 1, 1, 1),
-    ("cost", 2, 0, 3),
-    ("plan", 2, 0, 3),
-    ("cost", 2, 3, 3),
-    ("plan", 2, 3, 3),
-    ("cost", 3, 0, 6),
+    ("cost", 0, 0, 1), ("cost", 0, 2, 1), ("hub", 0, 0, 1), ("plan", 0, 0, 1),
+    ("cost", 0, 3, 2), ("plan", 0, 2, 1), ("plan", 0, 3, 2), ("scales", 0, 0, 0),
+    ("cost", 0, 5, 1), ("hub", 0, 1, 1), ("plan", 0, 5, 1), ("words", 0, 0, 2),
+    ("cost", 0, 1, 1), ("cost", 1, 0, 1), ("plan", 0, 1, 1), ("words", 0, 2, 2),
+    ("plan", 1, 0, 1), ("cost", 1, 2, 2), ("plan", 1, 2, 2), ("cost", 1, 4, 2),
+    ("plan", 1, 4, 2), ("cost", 1, 1, 1), ("plan", 1, 1, 1), ("cost", 2, 0, 3),
+    ("plan", 2, 0, 3), ("cost", 2, 3, 3), ("plan", 2, 3, 3), ("cost", 3, 0, 6),
     ("plan", 3, 0, 6),
 ]
-EMPTY_AT = [(7, 0, 0, 0), (8, 0, 1, 0), (9, 0, 0, 1), (8, 0, 1, 1), (14, 1, 0, 0), (14, 1, 1, 0), (15, 1, 0, 1), (15, 1, 1, 1), (20, 2, 0, 0), (20, 2, 1, 0), (21, 2, 0, 1), (21, 2, 1, 1)]
-SECOND_ON_VECTOR = (0, 3, 4, 5, 8, 9, 14, 15, 20, 21)
-POOL_FROM = 3
-SORT_FROM = 8
-LAST_LATE = 21
+
+LEAD = 2
+GPSIMD_FROM = 3
+SORT_FROM = 10
 
 
 def tile_transport_moment_step_s1_kernel(
@@ -82,10 +64,21 @@ def tile_transport_moment_step_s1_kernel(
     hub_rows = f_hub.rearrange("(g p t) d -> p g t d", p=P, t=PACK)
 
     units = [(pair, g, (0, 1)) for pair in range(PAIRS) for g in PASS_ORDER]
-    whole_units = len(units)
+    uncut = len(units)
     last_pair, last_pass, both = units.pop()
     units.extend((last_pair, last_pass, (r,)) for r in both)
     steps = len(units)
+
+    products = {}
+    for n, (pair, g, rs) in enumerate(units):
+        for r in rs:
+            for half in range(2):
+                slot = pair * PASSES + (SLOTS if pair else FIRST_SLOTS)[half][PASS_ORDER.index(g)]
+                if slot == steps - 2:
+                    slot = steps - 1
+                products.setdefault(min(slot, steps), []).append((n, r, half))
+    empties = {pair * PASSES + SLOTS[half][-1] + 1: (pair, half) for pair in range(PAIRS - 1) for half in range(2)}
+    scalar_busy = set(empties) | {s for s, engine in HUB_STEPS if s > 0}
 
     with ExitStack() as ctx:
         keep = ctx.enter_context(tc.tile_pool(name="keep", bufs=1))
@@ -116,7 +109,6 @@ def tile_transport_moment_step_s1_kernel(
         hub_raw = keep.tile([P, HUB_PASSES, PACK, D], BF16)
         rest_words = keep.tile([P, REST_PASSES, 2 * D], U8, align_bytes=64)
         loaded = {}
-
         for kind, pair, first, count in LOADS:
             if kind == "hub":
                 nc.sync.dma_start(out=hub_raw[:, first], in_=hub_rows[:, first])
@@ -148,7 +140,8 @@ def tile_transport_moment_step_s1_kernel(
         nc.vector.tensor_copy(out=step_col[:], in_=turned[:, 0:PASSES])
         nc.vector.tensor_tensor(out=stepv_col[:], in0=step_col[:], in1=turned[:, V_ROW : V_ROW + PASSES], op=ALU.mult)
 
-        slack, slack_t, plan_t, scaled, summed, clipped, codes, scales = {}, {}, {}, {}, {}, {}, {}, {}
+        slack, gate, sorted_words = {}, {}, {}
+        slack_t, plan_t, scaled, summed, clipped, codes, scales = {}, {}, {}, {}, {}, {}, {}
 
         def subtract(n, r, engine):
             pair, g, rs = units[n]
@@ -164,8 +157,6 @@ def tile_transport_moment_step_s1_kernel(
             else:
                 nc.gpsimd.tensor_scalar(out=dst, in0=src, scalar1=-1.0, scalar2=gate[n][:], op0=ALU.mult, op1=ALU.add)
 
-        gate, paired = {}, {}
-
         def open_gate(n):
             gate[n] = work.tile([P, 1], F32, name="gate", bufs=4)
             tile_no = 2 * units[n][0]
@@ -173,9 +164,10 @@ def tile_transport_moment_step_s1_kernel(
 
         def sort_words(n):
             pair, g, rs = units[n]
-            paired[pair, g] = work.tile([P, 2, 2, P], F32, name="paired", bufs=3)
+            sorted_words[n] = work.tile([P, 2, 2, P], F32, name="sorted_words", bufs=LEAD + 1)
             nc.vector.tensor_copy(
-                out=paired[pair, g][:], in_=loaded["plan", pair, g].bitcast(F32).rearrange("m r (p h) -> m r h p", h=2)
+                out=sorted_words[n][:],
+                in_=loaded["plan", pair, g].bitcast(F32).rearrange("m r (p h) -> m r h p", h=2),
             )
 
         def transpose(n):
@@ -193,8 +185,8 @@ def tile_transport_moment_step_s1_kernel(
             plan_t[n] = psum.tile([P, 2, len(rs) * P], F32, name="plan_bank", bufs=2)
             for h in range(2):
                 for place, r in enumerate(rs):
-                    if (pair, g) in paired:
-                        words = paired[pair, g][:, r, h, :]
+                    if n in sorted_words:
+                        words = sorted_words[n][:, r, h, :]
                     else:
                         words = loaded["plan", pair, g][:, r, :].bitcast(F32)[:, h : 2 * P : 2]
                     nc.tensor.transpose(plan_t[n][:, h, place * P : (place + 1) * P], words, ident[:])
@@ -243,21 +235,16 @@ def tile_transport_moment_step_s1_kernel(
         hub_codes = keep.tile([P, HUB_PASSES, D], U32, align_bytes=64)
         hub_scales = keep.tile([P, HUB_PASSES, D], U8, align_bytes=64)
 
-        def hub_pieces(at):
+        def hub_pieces(s):
+            found = []
             for piece, (piece_step, engine) in enumerate(HUB_STEPS):
-                if piece_step == at:
+                if piece_step == s:
                     g, part = divmod(piece, D // HUB_WIDTH)
-                    cols = slice(part * HUB_WIDTH, (part + 1) * HUB_WIDTH)
-                    hub_todo.append((piece, g, cols, engine))
+                    found.append((piece, g, slice(part * HUB_WIDTH, (part + 1) * HUB_WIDTH), engine))
+            return found
 
-        hub_todo = []
-
-        def interleave_hub(at, only=None):
-            hub_todo.clear()
-            hub_pieces(at)
-            for piece, g, cols, engine in hub_todo:
-                if only and engine != only:
-                    continue
+        def interleave_hub(s):
+            for piece, g, cols, engine in hub_pieces(s):
                 hub_grouped[piece] = work.tile([P, HUB_WIDTH, PACK], BF16, name="hub_grouped", bufs=4, align_bytes=64)
                 src = hub_raw[:, g, :, cols].rearrange("p t d -> p d t")
                 if engine == "scalar":
@@ -265,10 +252,8 @@ def tile_transport_moment_step_s1_kernel(
                 else:
                     nc.vector.tensor_copy(out=hub_grouped[piece][:], in_=src)
 
-        def quantise_hub(at):
-            hub_todo.clear()
-            hub_pieces(at)
-            for piece, g, cols, engine in hub_todo:
+        def quantise_hub(s):
+            for piece, g, cols, engine in hub_pieces(s):
                 nc.vector.quantize_mx(
                     out=hub_codes[:, g, cols].bitcast(FP8X4),
                     scales=hub_scales[:, g, cols],
@@ -307,50 +292,42 @@ def tile_transport_moment_step_s1_kernel(
                 nc.vector.tensor_copy(out=result[:], in_=acc[pair, r, half][:])
             nc.sync.dma_start(out=out_rows[:, 2 * pair + r, half * N_HALF : (half + 1) * N_HALF], in_=result[:])
 
-        products = {}
-        for n, (pair, g, rs) in enumerate(units):
-            for r in rs:
-                for half in range(2):
-                    slot = pair * PASSES + (SLOTS if pair else FIRST_SLOTS)[half][PASS_ORDER.index(g)]
-                    if slot == steps - 2:
-                        slot = steps - 1
-                    products.setdefault(min(slot, steps), []).append((n, r, half))
-
-        interleave_hub(-2)
         subtract(0, 0, "vector")
         subtract(0, 1, "scalar")
-        quantise_hub(-2)
         interleave_hub(-1)
         subtract(1, 0, "vector")
-        subtract(1, 1, "vector")
+        subtract(1, 1, "scalar")
         for s in range(steps):
-            ahead = s + 2 if s + 2 < whole_units else None
+            ahead = s + LEAD
             transpose(s)
             for item in sorted(products.get(s, [])):
                 multiply(*item)
             scale(s)
             add(s)
-            if 0 < s <= LAST_LATE + 1:
-                quantise(s - 1)
-            for at, pair, r, half in EMPTY_AT:
-                if at == s:
+            if s in empties:
+                pair, half = empties[s]
+                for r in range(2):
                     empty(pair, r, half, "scalar")
-            if ahead and ahead not in gate:
+            if 0 < s < steps - 1:
+                quantise(s - 1)
+            if ahead < GPSIMD_FROM:
                 subtract(ahead, 0, "vector")
-            if ahead:
-                subtract(ahead, 1, "vector" if s in SECOND_ON_VECTOR else "scalar")
-            if ahead and ahead >= SORT_FROM:
-                sort_words(ahead)
+            if ahead < uncut:
+                subtract(ahead, 1, "vector" if s in scalar_busy else "scalar")
+                if s >= SORT_FROM and s not in scalar_busy:
+                    sort_words(ahead)
             quantise_hub(s - 1)
-            for piece_engine in ("vector", "scalar"):
-                interleave_hub(s, piece_engine)
-            if POOL_FROM <= s + 3 < whole_units:
-                open_gate(s + 3)
-            clip(s)
-            if POOL_FROM <= s + 3 < whole_units:
-                subtract(s + 3, 0, "gpsimd")
-            if s > LAST_LATE:
-                quantise(s)
+            interleave_hub(s)
+            if ahead + 1 < uncut:
+                open_gate(ahead + 1)
+            if s < steps - 2:
+                clip(s)
+            if ahead + 1 < uncut:
+                subtract(ahead + 1, 0, "gpsimd")
+        for n in (steps - 2, steps - 1):
+            clip(n)
+        for n in (steps - 2, steps - 1):
+            quantise(n)
         for r in range(2):
             for half in range(2):
                 for item in sorted(products[steps]):

@@ -31,16 +31,18 @@ V_ROW = 8
 PASS_ORDER = [0, 2, 3, 4, 5, 1]
 
 HUB_WIDTH = 256
-HUB_STEPS = [(-1, "vector")] * 3 + [(0, "scalar")] + [(s, "scalar") for s in (3, 4, 5, 6)]
+HUB_STEPS = {3: (0, "vector"), 4: (3, "scalar"), 5: (4, "scalar"), 6: (5, "scalar"), 7: (6, "scalar")}
 
 SLOTS = ([3, 3, 4, 5, 6, 7], [4, 5, 6, 7, 8, 8])
-FIRST_SLOTS = ([3, 4, 5, 6, 7, 7], [4, 5, 6, 7, 8, 8])
+FIRST_SLOTS = ([2, 3, 4, 5, 6, 7], [3, 4, 5, 6, 8, 8])
+
+SPARE_PASSES = (6, 4)
 
 LOADS = [
-    ("cost", 0, 0, 1), ("cost", 0, 2, 1), ("hub", 0, 0, 1), ("plan", 0, 0, 1),
+    ("cost", 0, 0, 1), ("hub", 0, 0, 1), ("plan", 0, 0, 1), ("cost", 0, 2, 1),
     ("cost", 0, 3, 2), ("plan", 0, 2, 1), ("plan", 0, 3, 2), ("scales", 0, 0, 0),
-    ("cost", 0, 5, 1), ("hub", 0, 1, 1), ("plan", 0, 5, 1), ("words", 0, 0, 2),
-    ("cost", 0, 1, 1), ("cost", 1, 0, 1), ("plan", 0, 1, 1), ("words", 0, 2, 2),
+    ("words", 0, 0, 2), ("cost", 0, 5, 1), ("hub", 0, 1, 1), ("cost", 0, 1, 1),
+    ("plan", 0, 5, 1), ("cost", 1, 0, 1), ("plan", 0, 1, 1), ("words", 0, 2, 2),
     ("plan", 1, 0, 1), ("cost", 1, 2, 2), ("plan", 1, 2, 2), ("cost", 1, 4, 2),
     ("plan", 1, 4, 2), ("cost", 1, 1, 1), ("plan", 1, 1, 1), ("cost", 2, 0, 3),
     ("plan", 2, 0, 3), ("cost", 2, 3, 3), ("plan", 2, 3, 3), ("cost", 3, 0, 6),
@@ -78,7 +80,7 @@ def tile_transport_moment_step_s1_kernel(
                     slot = steps - 1
                 products.setdefault(min(slot, steps), []).append((n, r, half))
     empties = {pair * PASSES + SLOTS[half][-1] + 1: (pair, half) for pair in range(PAIRS - 1) for half in range(2)}
-    scalar_busy = set(empties) | {s for s, engine in HUB_STEPS if s > 0}
+    scalar_busy = set(empties) | {s for s, engine in HUB_STEPS.values() if engine == "scalar"}
 
     with ExitStack() as ctx:
         keep = ctx.enter_context(tc.tile_pool(name="keep", bufs=1))
@@ -136,9 +138,13 @@ def tile_transport_moment_step_s1_kernel(
         turned_bank = psum.tile([P, 2, 2, P], F32, name="plan_bank", bufs=2)
         for h in range(2):
             nc.tensor.transpose(turned_bank[:, h, 0, :], vectors[:].bitcast(F32)[:, h : 2 * P : 2], ident[:])
-        turned = turned_bank[:, :, 0, :].bitcast(BF16).rearrange("p h (g e) -> p g h e", e=2)
-        nc.vector.tensor_copy(out=step_col[:], in_=turned[:, 0:PASSES])
-        nc.vector.tensor_tensor(out=stepv_col[:], in0=step_col[:], in1=turned[:, V_ROW : V_ROW + PASSES], op=ALU.mult)
+
+        def fetch_columns():
+            turned = turned_bank[:, :, 0, :].bitcast(BF16).rearrange("p h (g e) -> p g h e", e=2)
+            nc.vector.tensor_copy(out=step_col[:], in_=turned[:, 0:PASSES])
+            nc.vector.tensor_tensor(
+                out=stepv_col[:], in0=step_col[:], in1=turned[:, V_ROW : V_ROW + PASSES], op=ALU.mult
+            )
 
         slack, gate, sorted_words = {}, {}, {}
         slack_t, plan_t, scaled, summed, clipped, codes, scales = {}, {}, {}, {}, {}, {}, {}
@@ -235,29 +241,41 @@ def tile_transport_moment_step_s1_kernel(
         hub_codes = keep.tile([P, HUB_PASSES, D], U32, align_bytes=64)
         hub_scales = keep.tile([P, HUB_PASSES, D], U8, align_bytes=64)
 
-        def hub_pieces(s):
-            found = []
-            for piece, (piece_step, engine) in enumerate(HUB_STEPS):
-                if piece_step == s:
-                    g, part = divmod(piece, D // HUB_WIDTH)
-                    found.append((piece, g, slice(part * HUB_WIDTH, (part + 1) * HUB_WIDTH), engine))
-            return found
+        def hub_place(piece):
+            g, part = divmod(piece, D // HUB_WIDTH)
+            return g, slice(part * HUB_WIDTH, (part + 1) * HUB_WIDTH)
 
-        def interleave_hub(s):
-            for piece, g, cols, engine in hub_pieces(s):
-                hub_grouped[piece] = work.tile([P, HUB_WIDTH, PACK], BF16, name="hub_grouped", bufs=4, align_bytes=64)
-                src = hub_raw[:, g, :, cols].rearrange("p t d -> p d t")
-                if engine == "scalar":
-                    nc.scalar.copy(out=hub_grouped[piece][:], in_=src)
-                else:
-                    nc.vector.tensor_copy(out=hub_grouped[piece][:], in_=src)
+        def interleave_hub(piece, engine):
+            g, cols = hub_place(piece)
+            hub_grouped[piece] = work.tile([P, HUB_WIDTH, PACK], BF16, name="hub_grouped", bufs=4, align_bytes=64)
+            dst = hub_grouped[piece][:].rearrange("p (c d) t -> p c t d", d=4)
+            src = hub_raw[:, g, :, cols].rearrange("p t (c d) -> p c t d", d=4)
+            if engine == "scalar":
+                nc.scalar.copy(out=dst, in_=src)
+            else:
+                nc.vector.tensor_copy(out=dst, in_=src)
 
-        def quantise_hub(s):
-            for piece, g, cols, engine in hub_pieces(s):
-                nc.vector.quantize_mx(
-                    out=hub_codes[:, g, cols].bitcast(FP8X4),
-                    scales=hub_scales[:, g, cols],
-                    in_=hub_grouped[piece][:].rearrange("p d t -> p (d t)"),
+        def quantise_hub(piece):
+            g, cols = hub_place(piece)
+            nc.vector.quantize_mx(
+                out=hub_codes[:, g, cols].bitcast(FP8X4),
+                scales=hub_scales[:, g, cols],
+                in_=hub_grouped[piece][:].rearrange("p d t -> p (d t)"),
+            )
+
+        spare_bank = psum.tile([P, N_HALF], F32, name="acc11")
+
+        def spare_passes(s):
+            g, cols = hub_place(0)
+            for repeat in range(SPARE_PASSES[s]):
+                nc.tensor.matmul_mx(
+                    out=spare_bank[:, cols],
+                    lhsT=hub_codes[:, g, 0:P].bitcast(FP8X4),
+                    lhsT_scale=hub_scales[:, g, 0:P],
+                    rhs=hub_codes[:, g, cols].bitcast(FP8X4),
+                    rhs_scale=hub_scales[:, g, cols],
+                    start=True,
+                    stop=True,
                 )
 
         acc = {}
@@ -292,23 +310,37 @@ def tile_transport_moment_step_s1_kernel(
                 nc.vector.tensor_copy(out=result[:], in_=acc[pair, r, half][:])
             nc.sync.dma_start(out=out_rows[:, 2 * pair + r, half * N_HALF : (half + 1) * N_HALF], in_=result[:])
 
-        subtract(0, 0, "vector")
-        subtract(0, 1, "scalar")
-        interleave_hub(-1)
+        subtract(0, 0, "scalar")
+        subtract(0, 1, "vector")
+        fetch_columns()
+        transpose(0)
+        interleave_hub(0, "vector")
+        quantise_hub(0)
+        interleave_hub(1, "vector")
         subtract(1, 0, "vector")
+        scale(0)
+        spare_passes(0)
+        quantise_hub(1)
         subtract(1, 1, "scalar")
+        add(0)
+        interleave_hub(2, "scalar")
+        quantise_hub(2)
+        clip(0)
         for s in range(steps):
             ahead = s + LEAD
-            transpose(s)
-            for item in sorted(products.get(s, [])):
-                multiply(*item)
-            scale(s)
-            add(s)
+            if s > 0:
+                transpose(s)
+                if s < len(SPARE_PASSES):
+                    spare_passes(s)
+                for item in sorted(products.get(s, []), key=lambda item: (item[0], item[2], item[1])):
+                    multiply(*item)
+                scale(s)
+                add(s)
             if s in empties:
                 pair, half = empties[s]
                 for r in range(2):
                     empty(pair, r, half, "scalar")
-            if 0 < s < steps - 1:
+            if 1 < s < steps - 1:
                 quantise(s - 1)
             if ahead < GPSIMD_FROM:
                 subtract(ahead, 0, "vector")
@@ -316,11 +348,16 @@ def tile_transport_moment_step_s1_kernel(
                 subtract(ahead, 1, "vector" if s in scalar_busy else "scalar")
                 if s >= SORT_FROM and s not in scalar_busy:
                     sort_words(ahead)
-            quantise_hub(s - 1)
-            interleave_hub(s)
+            for piece, (piece_step, engine) in sorted(HUB_STEPS.items()):
+                if piece_step == s - 1:
+                    quantise_hub(piece)
+                if piece_step == s:
+                    interleave_hub(piece, engine)
             if ahead + 1 < uncut:
                 open_gate(ahead + 1)
-            if s < steps - 2:
+            if s == 0:
+                quantise(0)
+            elif s < steps - 2:
                 clip(s)
             if ahead + 1 < uncut:
                 subtract(ahead + 1, 0, "gpsimd")

from contextlib import ExitStack

import concourse.mybir as mybir
from concourse.masks import make_identity

M, H, L, D = 1024, 1024, 2048, 1024
J = H + L
FLOPS = 2 * M * J * D

F32 = mybir.dt.float32
BF16 = mybir.dt.bfloat16
I32 = mybir.dt.int32
U32 = mybir.dt.uint32
U8 = mybir.dt.uint8
FP8X4 = mybir.dt.float8_e4m3fn_x4
FP4X4 = mybir.dt.float4_e2m1fn_x4
ALU = mybir.AluOpType
ACT = mybir.ActivationFunctionType

P = 128
PACK = 4
K_PASS = P * PACK
N_HALF = 512
TILES = M // P
PAIRS = TILES // 2
PASSES = J // K_PASS
HUB_PASSES = H // K_PASS
REST_PASSES = L // K_PASS
V_ROW = 8

PASS_ORDER = [0, 2, 3, 4, 5, 1]

HUB_WIDTH = 256
HUB_STEPS = {3: (0, "vector"), 4: (3, "scalar"), 5: (4, "scalar"), 6: (5, "scalar"), 7: (6, "scalar")}

SLOTS = ([3, 3, 4, 5, 6, 7], [4, 5, 6, 7, 8, 8])
FIRST_SLOTS = ([2, 3, 4, 5, 6, 7], [3, 4, 5, 6, 8, 8])

SPARE_PASSES = (6, 4)

LOADS = [
    ("cost", 0, 0, 1), ("hub", 0, 0, 1), ("plan", 0, 0, 1), ("cost", 0, 2, 1),
    ("cost", 0, 3, 2), ("plan", 0, 2, 1), ("plan", 0, 3, 2), ("scales", 0, 0, 0),
    ("words", 0, 0, 2), ("cost", 0, 5, 1), ("hub", 0, 1, 1), ("cost", 0, 1, 1),
    ("plan", 0, 5, 1), ("cost", 1, 0, 1), ("plan", 0, 1, 1), ("words", 0, 2, 2),
    ("plan", 1, 0, 1), ("cost", 1, 2, 2), ("plan", 1, 2, 2), ("cost", 1, 4, 2),
    ("plan", 1, 4, 2), ("cost", 1, 1, 1), ("plan", 1, 1, 1), ("cost", 2, 0, 3),
    ("plan", 2, 0, 3), ("cost", 2, 3, 3), ("plan", 2, 3, 3), ("cost", 3, 0, 6),
    ("plan", 3, 0, 6),
]

LEAD = 2
GPSIMD_FROM = 3
SORT_FROM = 10


def tile_transport_moment_step_s1_kernel(
    tc, plan, cost, u, v, step, f_hub, f_rest_words, f_rest_scales, out
):
    nc = tc.nc
    rows_of = {
        "plan": plan.rearrange("(m c) j -> m c j", c=TILES),
        "cost": cost.rearrange("(m c) j -> m c j", c=TILES),
    }
    out_rows = out.rearrange("(m c) d -> m c d", c=TILES)
    hub_rows = f_hub.rearrange("(g p t) d -> p g t d", p=P, t=PACK)

    units = [(pair, g, (0, 1)) for pair in range(PAIRS) for g in PASS_ORDER]
    uncut = len(units)
    last_pair, last_pass, both = units.pop()
    units.extend((last_pair, last_pass, (r,)) for r in both)
    steps = len(units)

    products = {}
    for n, (pair, g, rs) in enumerate(units):
        for r in rs:
            for half in range(2):
                slot = pair * PASSES + (SLOTS if pair else FIRST_SLOTS)[half][PASS_ORDER.index(g)]
                if slot == steps - 2:
                    slot = steps - 1
                products.setdefault(min(slot, steps), []).append((n, r, half))
    empties = {pair * PASSES + SLOTS[half][-1] + 1: (pair, half) for pair in range(PAIRS - 1) for half in range(2)}
    scalar_busy = set(empties) | {s for s, engine in HUB_STEPS.values() if engine == "scalar"}

    with ExitStack() as ctx:
        keep = ctx.enter_context(tc.tile_pool(name="keep", bufs=1))
        work = ctx.enter_context(tc.tile_pool(name="work", bufs=1))
        psum = ctx.enter_context(tc.psum_pool(name="psum", bufs=1))
        ctx.enter_context(tc.manual_schedule())

        vectors = keep.tile([P, K_PASS], BF16)
        nc.vector.memset(vectors[:].bitcast(I32), 0)
        u_col = keep.tile([P, TILES], BF16)
        nc.scalar.dma_start(out=u_col[:], in_=u.rearrange("(m c) -> m c", c=TILES))
        for lo, hi in ((0, 4), (4, PASSES)):
            nc.scalar.dma_start(out=vectors[lo:hi, :], in_=step.rearrange("(g k) -> g k", k=K_PASS)[lo:hi, :])
            nc.scalar.dma_start(
                out=vectors[V_ROW + lo : V_ROW + hi, :], in_=v.rearrange("(g k) -> g k", k=K_PASS)[lo:hi, :]
            )

        ident = keep.tile([P, P], F32)
        make_identity(nc, ident[:])

        rest_scales = keep.tile([P, REST_PASSES, D], U8, align_bytes=64)
        warm_in = keep.tile([P, 1], F32)
        warm_out = keep.tile([P, 1], F32)
        nc.vector.memset(warm_in[:], 0.0)
        nc.vector.memset(rest_scales[:].bitcast(I32), 0)
        nc.scalar.activation(out=warm_out[:], in_=warm_in[:], func=ACT.Identity, bias=warm_in[:], scale=-1.0)

        hub_raw = keep.tile([P, HUB_PASSES, PACK, D], BF16)
        rest_words = keep.tile([P, REST_PASSES, 2 * D], U8, align_bytes=64)
        loaded = {}
        for kind, pair, first, count in LOADS:
            if kind == "hub":
                nc.sync.dma_start(out=hub_raw[:, first], in_=hub_rows[:, first])
            elif kind == "words":
                groups = slice(first, first + count)
                nc.sync.dma_start(
                    out=rest_words[:, groups, :].bitcast(I32),
                    in_=f_rest_words[groups].rearrange("g p n -> p g n").bitcast(I32),
                )
            elif kind == "scales":
                for quad in range(4):
                    nc.sync.dma_start(
                        out=rest_scales[32 * quad : 32 * quad + 4, :, :].bitcast(I32),
                        in_=f_rest_scales[:, 4 * quad : 4 * quad + 4, :].rearrange("g r n -> r g n").bitcast(I32),
                    )
            else:
                cols = slice(first * K_PASS, (first + count) * K_PASS)
                chunk = keep.tile([P, 2, count * K_PASS], BF16, name="%s%d_%d" % (kind, pair, first))
                nc.sync.dma_start(out=chunk[:], in_=rows_of[kind][:, 2 * pair : 2 * pair + 2, cols])
                for g in range(first, first + count):
                    loaded[kind, pair, g] = chunk[:, :, (g - first) * K_PASS : (g - first + 1) * K_PASS]

        step_col = keep.tile([P, PASSES, 2, 2], F32)
        stepv_col = keep.tile([P, PASSES, 2, 2], F32)
        turned_bank = psum.tile([P, 2, 2, P], F32, name="plan_bank", bufs=2)
        for h in range(2):
            nc.tensor.transpose(turned_bank[:, h, 0, :], vectors[:].bitcast(F32)[:, h : 2 * P : 2], ident[:])

        def fetch_columns():
            turned = turned_bank[:, :, 0, :].bitcast(BF16).rearrange("p h (g e) -> p g h e", e=2)
            nc.vector.tensor_copy(out=step_col[:], in_=turned[:, 0:PASSES])
            nc.vector.tensor_tensor(
                out=stepv_col[:], in0=step_col[:], in1=turned[:, V_ROW : V_ROW + PASSES], op=ALU.mult
            )

        slack, gate, sorted_words = {}, {}, {}
        slack_t, plan_t, scaled, summed, clipped, codes, scales = {}, {}, {}, {}, {}, {}, {}

        def subtract(n, r, engine):
            pair, g, rs = units[n]
            if (pair, g) not in slack:
                slack[pair, g] = work.tile([P, 2, PACK, P], F32, name="slack", bufs=4)
            dst = slack[pair, g][:, r]
            src = loaded["cost", pair, g][:, r, :].rearrange("m (p t) -> m t p", t=PACK)
            u_here = u_col[:, 2 * pair + r : 2 * pair + r + 1]
            if engine == "scalar":
                nc.scalar.activation(out=dst, in_=src, func=ACT.Identity, bias=u_here, scale=-1.0)
            elif engine == "vector":
                nc.vector.tensor_scalar(out=dst, in0=src, scalar1=-1.0, scalar2=u_here, op0=ALU.mult, op1=ALU.add)
            else:
                nc.gpsimd.tensor_scalar(out=dst, in0=src, scalar1=-1.0, scalar2=gate[n][:], op0=ALU.mult, op1=ALU.add)

        def open_gate(n):
            gate[n] = work.tile([P, 1], F32, name="gate", bufs=4)
            tile_no = 2 * units[n][0]
            nc.vector.tensor_copy(out=gate[n][:], in_=u_col[:, tile_no : tile_no + 1])

        def sort_words(n):
            pair, g, rs = units[n]
            sorted_words[n] = work.tile([P, 2, 2, P], F32, name="sorted_words", bufs=LEAD + 1)
            nc.vector.tensor_copy(
                out=sorted_words[n][:],
                in_=loaded["plan", pair, g].bitcast(F32).rearrange("m r (p h) -> m r h p", h=2),
            )

        def transpose(n):
            pair, g, rs = units[n]
            per_bank = PACK // len(rs)
            slack_t[n] = []
            for t in range(PACK):
                if t % per_bank == 0:
                    bank = psum.tile([P, per_bank, len(rs) * P], F32, name="slack_bank", bufs=2)
                for place, r in enumerate(rs):
                    nc.tensor.transpose(
                        bank[:, t % per_bank, place * P : (place + 1) * P], slack[pair, g][:, r, t, :], ident[:]
                    )
                slack_t[n].append(bank[:, t % per_bank, :])
            plan_t[n] = psum.tile([P, 2, len(rs) * P], F32, name="plan_bank", bufs=2)
            for h in range(2):
                for place, r in enumerate(rs):
                    if n in sorted_words:
                        words = sorted_words[n][:, r, h, :]
                    else:
                        words = loaded["plan", pair, g][:, r, :].bitcast(F32)[:, h : 2 * P : 2]
                    nc.tensor.transpose(plan_t[n][:, h, place * P : (place + 1) * P], words, ident[:])

        def scale(n):
            pair, g, rs = units[n]
            scaled[n] = work.tile([P, 2, 2, len(rs) * P], F32, name="scaled", bufs=3)
            for t in range(PACK):
                h, e = divmod(t, 2)
                nc.scalar.activation(
                    out=scaled[n][:, h, e, :],
                    in_=slack_t[n][t],
                    func=ACT.Identity,
                    bias=stepv_col[:, g, h, e : e + 1],
                    scale=step_col[:, g, h, e : e + 1],
                )

        def add(n):
            width = len(units[n][2]) * P
            summed[n] = work.tile([P, 2, width, 2], BF16, name="summed", bufs=3)
            nc.vector.tensor_tensor(
                out=summed[n][:],
                in0=scaled[n][:].rearrange("p h e i -> p h i e"),
                in1=plan_t[n][:].bitcast(BF16).rearrange("p h (i e) -> p h i e", e=2),
                op=ALU.add,
            )

        def clip(n):
            width = len(units[n][2]) * P
            clipped[n] = work.tile([P, width, 2, 2], BF16, name="clipped", bufs=3, align_bytes=64)
            nc.vector.tensor_scalar_max(
                out=clipped[n][:], in0=summed[n][:].rearrange("p h i e -> p i h e"), scalar1=0.0
            )

        def quantise(n):
            width = len(units[n][2]) * P
            codes[n] = work.tile([P, width], U32, name="codes", bufs=8, align_bytes=64)
            scales[n] = work.tile([P, width], U8, name="scales", bufs=8, align_bytes=64)
            nc.vector.quantize_mx(
                out=codes[n][:].bitcast(FP8X4),
                scales=scales[n][:],
                in_=clipped[n][:].rearrange("p i h e -> p (i h e)"),
            )

        hub_grouped = {}
        hub_codes = keep.tile([P, HUB_PASSES, D], U32, align_bytes=64)
        hub_scales = keep.tile([P, HUB_PASSES, D], U8, align_bytes=64)

        def hub_place(piece):
            g, part = divmod(piece, D // HUB_WIDTH)
            return g, slice(part * HUB_WIDTH, (part + 1) * HUB_WIDTH)

        def interleave_hub(piece, engine):
            g, cols = hub_place(piece)
            hub_grouped[piece] = work.tile([P, HUB_WIDTH, PACK], BF16, name="hub_grouped", bufs=4, align_bytes=64)
            dst = hub_grouped[piece][:].rearrange("p (c d) t -> p c t d", d=4)
            src = hub_raw[:, g, :, cols].rearrange("p t (c d) -> p c t d", d=4)
            if engine == "scalar":
                nc.scalar.copy(out=dst, in_=src)
            else:
                nc.vector.tensor_copy(out=dst, in_=src)

        def quantise_hub(piece):
            g, cols = hub_place(piece)
            nc.vector.quantize_mx(
                out=hub_codes[:, g, cols].bitcast(FP8X4),
                scales=hub_scales[:, g, cols],
                in_=hub_grouped[piece][:].rearrange("p d t -> p (d t)"),
            )

        spare_bank = psum.tile([P, N_HALF], F32, name="acc11")

        def spare_passes(s):
            g, cols = hub_place(0)
            for repeat in range(SPARE_PASSES[s]):
                nc.tensor.matmul_mx(
                    out=spare_bank[:, cols],
                    lhsT=hub_codes[:, g, 0:P].bitcast(FP8X4),
                    lhsT_scale=hub_scales[:, g, 0:P],
                    rhs=hub_codes[:, g, cols].bitcast(FP8X4),
                    rhs_scale=hub_scales[:, g, cols],
                    start=True,
                    stop=True,
                )

        acc = {}

        def multiply(n, r, half):
            pair, g, rs = units[n]
            rows = slice(rs.index(r) * P, (rs.index(r) + 1) * P)
            cols = slice(half * N_HALF, (half + 1) * N_HALF)
            if g == PASS_ORDER[0]:
                acc[pair, r, half] = psum.tile([P, N_HALF], F32, name="acc%d%d" % (r, half))
            if g < HUB_PASSES:
                rhs = hub_codes[:, g, cols].bitcast(FP8X4)
                rhs_scale = hub_scales[:, g, cols]
            else:
                rhs = rest_words[:, g - HUB_PASSES, half * 2 * N_HALF : (half + 1) * 2 * N_HALF].bitcast(FP4X4)
                rhs_scale = rest_scales[:, g - HUB_PASSES, cols]
            nc.tensor.matmul_mx(
                out=acc[pair, r, half][:],
                lhsT=codes[n][:, rows].bitcast(FP8X4),
                lhsT_scale=scales[n][:, rows],
                rhs=rhs,
                rhs_scale=rhs_scale,
                start=(g == PASS_ORDER[0]),
                stop=(g == PASS_ORDER[-1]),
            )

        def empty(pair, r, half, engine):
            result = work.tile([P, N_HALF], F32, name="result", bufs=6)
            if engine == "scalar":
                nc.scalar.copy(out=result[:], in_=acc[pair, r, half][:])
            else:
                nc.vector.tensor_copy(out=result[:], in_=acc[pair, r, half][:])
            nc.sync.dma_start(out=out_rows[:, 2 * pair + r, half * N_HALF : (half + 1) * N_HALF], in_=result[:])

        subtract(0, 0, "scalar")
        subtract(0, 1, "vector")
        fetch_columns()
        transpose(0)
        interleave_hub(0, "vector")
        quantise_hub(0)
        interleave_hub(1, "vector")
        subtract(1, 0, "vector")
        scale(0)
        spare_passes(0)
        quantise_hub(1)
        subtract(1, 1, "scalar")
        add(0)
        interleave_hub(2, "scalar")
        quantise_hub(2)
        clip(0)
        for s in range(steps):
            ahead = s + LEAD
            if s > 0:
                transpose(s)
                if s < len(SPARE_PASSES):
                    spare_passes(s)
                for item in sorted(products.get(s, []), key=lambda item: (item[0], item[2], item[1])):
                    multiply(*item)
                scale(s)
                add(s)
            if s in empties:
                pair, half = empties[s]
                for r in range(2):
                    empty(pair, r, half, "scalar")
            if 1 < s < steps - 1:
                quantise(s - 1)
            if ahead < GPSIMD_FROM:
                subtract(ahead, 0, "vector")
            if ahead < uncut:
                subtract(ahead, 1, "vector" if s in scalar_busy else "scalar")
                if s >= SORT_FROM and s not in scalar_busy:
                    sort_words(ahead)
            for piece, (piece_step, engine) in sorted(HUB_STEPS.items()):
                if piece_step == s - 1:
                    quantise_hub(piece)
                if piece_step == s:
                    interleave_hub(piece, engine)
            if ahead + 1 < uncut:
                open_gate(ahead + 1)
            if s == 0:
                quantise(0)
            elif s < steps - 2:
                clip(s)
            if ahead + 1 < uncut:
                subtract(ahead + 1, 0, "gpsimd")
        for n in (steps - 2, steps - 1):
            clip(n)
        for n in (steps - 2, steps - 1):
            quantise(n)
        for r in range(2):
            for half in range(2):
                for item in sorted(products[steps]):
                    if item[1:] == (r, half):
                        multiply(*item)
                empty(PAIRS - 1, r, half, "vector" if half else "scalar")
